import numpy as np, ml_dtypes
CORES = [6,15,38,47]
N = 4
BF = ml_dtypes.bfloat16
def gentries(a):
    return np.ascontiguousarray(a.reshape(8, 16, -1).transpose(0, 2, 1)).reshape(8, -1)
def gtable(e):
    e = np.asarray(e); return np.ascontiguousarray(e.reshape(8, -1, 16).transpose(0, 2, 1)).reshape(128, -1).astype(np.int32)
W, LW, C, B, KEYS, Q, RO = 4096, 12, 256, 16, 16, 9, 3
def pick(T, c):
    L = np.ascontiguousarray(c.transpose(0, 1, 3, 2)).reshape(N * 8, 16 * C)
    return np.stack([np.take(a, l, axis=1) for a, l in zip(T.reshape(N * 8, 16, W), L)]).reshape(N, 8, 16, C, 16)
def ask(D, X, c, y, w):
    d = pick(D, c); same = (d & (KEYS - 1)) == (c & (KEYS - 1))[..., None]
    cp = np.maximum(c, np.max(np.where(same, d, 0), axis=4))
    x = pick(X, cp); z = (np.max(x, axis=4) + np.min(x, axis=4)) >> 1
    u = np.add.reduce(w * z, axis=2, keepdims=True) & 4095
    return cp, z, u, B * np.arange(C) + (u & (B - 1)), np.abs(z - y)
def put(T, pl, val):
    np.put_along_axis(T, pl, val, axis=3)
def far(X, cp, v):
    return np.add.reduce(np.abs(pick(X, cp) - v[..., None]), axis=2)
def eve(D, X, c, y, w):
    cp, z, u, pl, v = ask(D, X, c, y, w); X = X.copy(); put(X, pl, v)
    return np.sort(far(X, np.roll(cp, 1, axis=0), np.roll(v, 1, axis=0)), axis=-1)[..., Q - 1]
def level(rng, q):
    return np.take_along_axis(np.sort(q, axis=-1), rng.integers(C // 4, 3 * C // 4, (N, 8, 1)), 2)[..., 0]
def sums(rng, tot):
    a = (tot[:, None, :] + np.arange(16).reshape(16, 1)) >> 4; hi, lo = a[:, :8], a[:, 8:]
    e = np.floor(rng.random((N, 8, C)) * (np.minimum(255 - hi, lo) + 1)).astype(np.int64)
    return rng.permuted(np.concatenate([hi + e, lo - e], axis=1), axis=1)
def parts(rng):
    D = rng.integers(0, W, (N, 8, 16, W)); X = (rng.random((N, 8, 16, W)) * rng.integers(64, 257, (N, 8, 1, W))).astype(np.int64)
    c = rng.integers(0, W, (N, 8, 16, C)); y = rng.integers(0, 256, (N, 8, 16, C)); w = rng.integers(0, 16, (N, 8, 16, C)); m = rng.integers(0, 2048, (N, 8, 16, 1))
    return D, X, c, y, w, m
def pack(D, X, c, y, w, m, th):
    return {"rec": (W * X + D).reshape(N, 128, W).astype(np.int32), "req": np.stack([gtable(a.transpose(0, 2, 1).reshape(8, 16 * C)) for a in c]),
            "aim": y.reshape(N, 128, C).astype(np.float32).astype(BF), "wt": w.reshape(N, 128, C).astype(np.float32).astype(BF),
            "mul": m.reshape(N, 128, 1).astype(np.int32), "th": np.repeat(th, 16, axis=1).reshape(N, 128, 1).astype(np.int32)}
def setup_inputs(rng):
    D, X, c, y, w, m = parts(rng)
    return pack(D, X, c, y, w, m, level(rng, eve(D, X, c, y, w)))
def setup_inputs_ties(rng):
    D, X, c, y, w, m = parts(rng); h = C // 2
    put(D, c[..., h:], (c[..., h:] + KEYS) & (W - 1)); put(D, c[..., :h], c[..., :h])
    z = ask(D, X, c, y, w)[1]
    y = np.where(rng.random((N, 8, 1, C)) < 0.3, np.minimum(np.maximum(z + rng.integers(-1, 2, z.shape), 0), 255), y)
    th = level(rng, eve(D, X, c, y, w)) + ((np.arange(8) + np.arange(N)[:, None]) & 1)
    return pack(D, X, c, y, w, m, th)
def setup_inputs_alike(rng):
    D, X, c, y, w, m = parts(rng)
    D[:, 1::2] += KEYS // 2 - (D[:, 1::2] & (KEYS - 1)); c[:, 1::2] += KEYS // 2 - (c[:, 1::2] & (KEYS - 1))
    c[:, 0] = rng.choice(np.array([0, W - 1, W // 2, 5]), (N, 16, C)); c[:, 4] = rng.choice(np.array([0, W - 1, W - 2, KEYS - 1, 7 * KEYS - 1]), (N, 16, C)); c[:, 6] = c[:, 6, :1]
    D[:, 2] = np.arange(W); D[:, 4] = W - 1; D[:, 6] = 0
    X[:, 4] = 255 * rng.integers(0, 2, (N, 1, W))
    return pack(D, X, c, y, w, m, level(rng, eve(D, X, c, y, w)))
def setup_inputs_ends(rng):
    D, X, c, y, w, m = parts(rng)
    th = rng.choice(np.array([0, 1, 4080, 4081]), (N, 8)); q = rng.permutation(N); th[q[0]] = 4081; th[q[1]] = 0
    w[:, 1] = 0
    X[:, 3, :2] = 255; X[:, 3, 2] = 15; w[:, 3] = 0; w[:, 3, 0] = 15; w[:, 3, 1:3] = 1; m[:, 3] = 2047
    y[:, 5] = 255 * rng.integers(0, 2, (N, 16, C)); w[:, 5] = 15; m[:, 5] = 0
    X[:, 7] = 255; y[:, 7] = 255; th[:, 7] = 4080 + (np.arange(N) & 1)
    return pack(D, X, c, y, w, m, th)
def setup_inputs_own(rng):
    D, X, c, y, w, m = parts(rng); lim = 4 * int(rng.integers(513, 1000)) + int(rng.integers(0, 2))
    X[:, :2, :, 1::2] = 255; c[:, :2] |= 1; w[:, :2] = w[:, :2, :1]
    y[:, 0] = sums(rng, rng.choice(np.array([0, 0, 1, 16]), (N, C))); y[:, 1] = sums(rng, lim + rng.integers(-2, 2, (N, C)))
    X[:, 2] = 255 - rng.integers(0, 17, (N, 16, W)); w[:, 2] = 14 + rng.integers(0, 2, (N, 16, C)); y[:, 2] = y[:, 2] * rng.integers(0, 2, (N, 1, C))
    for g, h in ((3, 127), (4, C - 1), (5, int(rng.choice(np.array([32, 63, 64, C // 2, C - 2]))))):
        D[:, g] = B * h; w[:, g] = 0; c[:, g] = KEYS * rng.integers(0, B * h // KEYS + 1, (N, 16, C))
        b = np.tile(rng.integers(0, 2, (1, 16)), (N, 1)); b[np.arange(N), rng.permutation(16)[:N]] ^= 1
        X[:, g, :, B * h] = KEYS * b; y[:, g] = KEYS * rng.integers(0, 2, (N, 16, C)); y[:, g, :, h] = KEYS
    c[:, 6, :, ::2] = 0; D[:, 6, :, 0] = 0; X[:, 6, :, 0] = 0; y[:, 6, :, 0] = 0
    D[:, 7] = np.arange(W); c[:, 7] = (B * (np.arange(C) + rng.integers(-1, 2, (N, 16, C))) + rng.integers(0, B, (N, 16, C))) & (W - 1)
    th = level(rng, eve(D, X, c, y, w))
    th[:, 0] = (np.arange(N) + int(rng.integers(0, 2))) & 1; th[:, 1] = lim; th[:, 3:6] = 8 * KEYS; th[:, 6] = rng.integers(1900, 2200, N)
    return pack(D, X, c, y, w, m, th)
def setup_inputs_spread(rng):
    D, X, c, y, w, m = parts(rng)
    def uneven(*shape):
        a = np.exp2(LW * rng.random(shape)).astype(np.int64) - 1
        return np.where(rng.random(shape[:-2] + (1, shape[-1])) < 0.5, a, W - 1 - a)
    D = np.where(rng.random((N, 8, 1, W)) < 0.5, uneven(N, 8, 16, W), D); c = np.where(rng.random((N, 8, 1, C)) < 0.5, uneven(N, 8, 16, C), c)
    X = (np.exp2(8 * rng.random((N, 8, 1, W))) * rng.random((N, 8, 16, W))).astype(np.int64)
    y = (np.exp2(8 * rng.random((N, 8, 1, C))) * rng.random((N, 8, 16, C))).astype(np.int64); w = w * (rng.random(w.shape) < rng.random((N, 8, 1, C)))
    m = (np.exp2(11 * rng.random(m.shape))).astype(np.int64)
    return pack(D, X, c, y, w, np.minimum(m, 2047), level(rng, eve(D, X, c, y, w)))
def check_inputs(d):
    bad = []
    for k, lo, hi in (("rec", 0, 256 * W - 1), ("req", 0, W - 1), ("aim", 0, 255), ("wt", 0, 15), ("mul", 0, 2047), ("th", 0, 4081)):
        a = np.asarray(d[k]).astype(np.float64)
        if not (np.min(a) >= lo and np.max(a) <= hi): bad.append("range of " + k)
        if not np.all(a == np.floor(a)): bad.append("whole numbers in " + k)
    a = np.asarray(d["th"]).reshape(N, 8, 16)
    if np.any(a != a[:, :, :1]): bad.append("th alike in the rows of a group")
    return bad
def reference(rec, req, aim, wt, mul, th):
    R = rec.astype(np.int64).reshape(N, 8, 16, W); D = R & (W - 1); X = R >> LW
    c = req.astype(np.int64).reshape(N, 8, 16, C)
    y = aim.astype(np.int64).reshape(N, 8, 16, C); w = wt.astype(np.int64).reshape(N, 8, 16, C)
    m = mul.astype(np.int64).reshape(N, 8, 16, 1); lim = th.astype(np.int64).reshape(N, 8, 16)[:, :, 0]
    odd = 2 * np.arange(16).reshape(16, 1) + 1
    for t in range(RO):
        cp, z, u, pl, v = ask(D, X, c, y, w)
        put(D, pl, cp); put(X, pl, v)
        sh = 1 + t % (N - 1)
        ca = np.roll(cp, sh, axis=0); va = np.roll(v, sh, axis=0); pa = np.roll(pl, sh, axis=0)
        near = np.add.reduce((far(X, ca, va) < lim[:, :, None, None]).astype(np.int64), axis=3)
        ok = (near >= Q)[:, :, None, :]
        put(D, pa, np.where(ok, ca, np.take_along_axis(D, pa, 3))); put(X, pa, np.where(ok, va, np.take_along_axis(X, pa, 3)))
        c = (((u * u) >> 5) + m * u + odd * z) & (W - 1)
    return {"yc": c.reshape(N, 128, C).astype(np.float32), "yz": z.reshape(N, 128, C).astype(np.float32).astype(BF), "yx": X.reshape(N, 128, W).astype(np.float32).astype(BF)}

from concourse.mybir import dt, AluOpType, AxisListType, ActivationFunctionType

A = AluOpType
F = ActivationFunctionType
STEPS = 3
W = 4096
WP = W + 256
C1 = [(0, 64), (64, 128), (128, 192), (192, 256)]
C3 = [(0, 64), (64, 128), (128, 192), (192, 256)]
SC = {128: 0, 256: 128}
SV = {128: 0, 256: 128}
AC = (2,)
KG = {2: 0, 3: 3}
BC0 = [(0, 128, "v"), (128, 256, "g")]
BCN = [(0, 128, "v"), (128, 256, "g")]
UNP = [512, 512, 1024, 1024, 1024]
GAM, SCT, CYC, PEC, LAT, WIN = 1.5, 3.5, 0.000833, 0.00042, 0.08, 0.2
SND, ARR = 1.2, 3.5
PRI = {"vMXA.12": -1, "vMN.12": -3, "vU1.12": -5, "vWZ.0": -5, "sHB.512": 5, "sHB.3072": 6, "gCKB.8": -11, "sHB.2048": 6,
       "sA1.3584": 8, "sHB.2560": -1, "vMX.12": -4, "vMI.12": -5, "vTT.4": -6, "tps3.6": 5, "sXX.3": 12, "tps3.14": -7,
       "sXG.12": -12, "vZ.8": -9, "vZ.4": 4, "vZ.12": -15, "vCP.12": -6, "sVN.0": -10, "tps4.24": 5}
ORDER = {}

SCRATCH = {"b%d" % _b: ("psum", [128, 512], "float32") for _b in range(8)}


def _sb(cols, dtype, names):
    for n in names.split():
        SCRATCH[n] = ("sbuf", [128, cols], dtype)


_sb(W, "int32", "REC")
_sb(W, "float32", "A2 D7 A1")
_sb(W, "bfloat16", "HB CKB U1 AB MN XG MX MI XA MXA")
_sb(WP, "float32", "TT")
_sb(WP, "bfloat16", "XX")
_sb(256, "int32", "REQ RP CC KK A32 UI UU SQ FF")
_sb(256, "bfloat16", "AIM WT KM M2 Z H16 HZ FL")
_sb(256, "float16", "WZ UM C2K")
_sb(256, "float32", "YC")
_sb(256, "uint16", "C16")
_sb(1, "int32", "MUL TH")
_sb(1, "float32", "THH KF ODC")
_sb(2048, "bfloat16", "ONES SELA SELC SELB SELM")
_sb(2048, "float16", "SELH")
_sb(128, "bfloat16", "BM0 BM BMH IDP IDN IDK IDM IDH IDQ ID4 ID7 OD")
_sb(128, "float16", "KD BH")
_sb(1024, "bfloat16", "MSN MSX")
_sb(16, "int32", "PRI PR I256 I16 R16 N32 N15")
_sb(16, "float32", "BASE DUM DMC PDC PI PD OF OG")
_sb(16, "uint16", "P16 O16")
for _t in range(STEPS):
    _sb(256, "uint16", "CP%d CA%d" % (_t, _t))
    _sb(256, "float32", "TV%d TA%d" % (_t, _t))
    _sb(272, "bfloat16", "VN%d VA%d" % (_t, _t))
SEMAPHORES = ["sv", "ss", "st", "sg"] + ["d%d" % k for k in range(16)] + \
    ["%s%d%s" % (m, t, x) for m in ("c", "e", "t", "v", "w") for t in range(STEPS) for x in ("l", "r")]


def tk(name, lo, hi):
    return [(name, u) for u in range(lo // 16, (hi + 15) // 16)]


def plan(ops):
    lw, rd, bk = {}, {}, {}
    preds = []
    for i in range(len(ops)):
        o = ops[i]
        d = {}

        def need(j, sync):
            if j != i:
                d[j] = d.get(j, False) or sync
        for j in o["after"]:
            need(j, False)
        for r in o["R"]:
            if r in lw:
                need(lw[r], True)
        for w in o["W"]:
            if w in lw:
                need(lw[w], True)
            for j in rd.get(w, ()):
                need(j, ops[j]["e"] != o["e"] or ops[j]["k"] != "c")
        for b in o["B"]:
            for e, j in bk.get(b, {}).items():
                need(j, e != o["e"])
        for r in o["R"]:
            rd.setdefault(r, []).append(i)
        for w in o["W"]:
            lw[w] = i
            rd[w] = []
        for b in o["B"]:
            bk.setdefault(b, {})[o["e"]] = i
        preds.append(d)
    return preds


def schedule(ops, preds):
    n = len(ops)
    succ = [[] for _ in range(n)]
    for i in range(n):
        for j in preds[i]:
            succ[j].append(i)
    bl = [0.0] * n
    for i in range(n - 1, -1, -1):
        bl[i] = ops[i]["dur"] + max([bl[j] + LAT for j in succ[i]] + [0.0])
    bl = [bl[i] + PRI.get(ops[i]["tag"], 0.0) for i in range(n)]
    cnt = [len(preds[i]) for i in range(n)]
    rdy = [0.0] * n
    free = {}
    avail = [i for i in range(n) if cnt[i] == 0]
    order, start = [], [0.0] * n
    end = 0.0
    while avail:
        best = None
        for i in avail:
            s = max(rdy[i], free.get(ops[i]["e"], 0.0))
            if best is None or s < best:
                best, e = s, ops[i]["e"]
        c = [i for i in avail if ops[i]["e"] == e and max(rdy[i], free.get(e, 0.0)) <= best + WIN]
        i = max(c, key=lambda x: (bl[x], -x))
        avail.remove(i)
        s = max(rdy[i], free.get(e, 0.0))
        start[i] = s
        if e != "n":
            free[e] = s + ops[i]["occ"]
        f = s + ops[i]["dur"]
        end = max(end, f)
        order.append(i)
        for j in succ[i]:
            cnt[j] -= 1
            rdy[j] = max(rdy[j], f + LAT if preds[j][i] else s)
            if cnt[j] == 0:
                avail.append(j)
    return order, start, end


def build(g, T, core, topo):
    ops = []
    q = {"v": g.vector, "s": g.scalar, "t": g.tensor, "g": g, "y": g.sync}
    t_ = T

    def add(e, calls, cost, R, W_, B=(), k="c", occ=None, sem=None, val=0, after=()):
        R, W_ = list(R), list(W_)
        w0 = W_[0]
        if isinstance(w0, tuple):
            u = w0[1]
            nm = w0[0] if isinstance(w0[0], str) else w0[0][0]
            if nm == "ps":
                nm = "ps%d" % u
                u = len(calls) + (sorted(x[1] for x in R if x[0] in ("M2", "MX", "Z", "WZ", "XA", "MXA", "FL")) + [0])[0]
            w0 = "%s.%s" % (nm, u)
        ops.append({"tag": e + w0, "e": e, "f": calls, "dur": cost, "occ": cost if occ is None else occ, "R": R, "W": W_,
                    "B": list(B), "k": k, "sem": sem, "val": val, "after": list(after)})

    def vts(out, i, s1, s2, op0, op1, n, R, W_, B=(), rate=1.0):
        if op1 is None:
            f = lambda: g.vector.tensor_scalar(out, i, s1, None, op0)
        else:
            f = lambda: g.vector.tensor_scalar(out, i, s1, s2, op0, op1)
        add("v", [f], max(64, n * rate) * CYC, R, W_, B)

    def vtt(out, a, b, op, n, R, W_, B=(), rate=2.0):
        add("v", [lambda: g.vector.tensor_tensor(out, a, b, op)], max(64, n * rate) * CYC, R, W_, B)

    def vcp(out, i, n, R, W_, B=(), rate=1.0):
        add("v", [lambda: g.vector.tensor_copy(out, i)], max(64, n * rate) * CYC, R, W_, B)

    def vset(ap, c, n, W_):
        add("v", [lambda: g.vector.memset(ap, c)], max(64, n) * CYC, (), W_)

    def vscan(out, m, i, op0, op1, n, R, W_):
        add("v", [lambda: g.vector.tensor_tensor_scan(out, m, i, 0.0, op0, op1)], n * 0.5 * CYC, R, W_)

    def act(out, i, fn, n, R, W_, B=(), bias=0.0, scale=1.0):
        add("s", [lambda: g.scalar.activation(out, i, fn, bias=bias, scale=scale)], max(64, n) * CYC + 0.02, R, W_, B)

    def sgat(out, i, n, R, W_):
        add("s", [lambda: g.scalar.activation(out, i, F.Copy)], n * GAM * CYC + 0.065, R, W_)

    def vscat(out, i, n, R, W_):
        add("v", [lambda: g.vector.tensor_copy(out, i)], n * SCT * CYC + 0.05, R, W_)

    def mm(lst, R, b):
        fs = [(lambda o=o, l=l, r=r, s=s, p=p: g.tensor.matmul(o, l, r, s, p)) for (o, l, r, n, s, p) in lst]
        add("t", fs, sum(max(64, x[3]) for x in lst) * PEC + 0.03, R, [("ps", b)], [b])

    nd = [0]

    def dma(e, out, i, cost, R, W_):
        s = "d%d" % nd[0]
        nd[0] += 1
        add(e, [lambda: q[e].dma_start(out, i)], cost, R, W_, (), "d", 0.1, s, 16)

    def spread(lo, hi, e):
        n = hi - lo
        fs = []
        for j in range(16):
            o, i = t_.CKB[:, 16 * lo + j:16 * hi:16], t_.KM[:, lo:hi]
            if e == "v":
                fs.append(lambda o=o, i=i: g.vector.tensor_copy(o, i))
            else:
                fs.append(lambda o=o, i=i: g.affine_select(o, i, [[0, n]], A.is_equal, 0.0, 0, 0))
        c = {"v": max(64, n * 0.5) * CYC, "g": 0.17 + 2 * n * CYC}[e]
        add(e, fs, 16 * c, tk("KM", lo, hi), tk("CKB", lo, hi))

    UB = [sum(UNP[:k]) for k in range(len(UNP) + 1)]
    dma("y", t_.REQ[:], t_.req[:], 2.2, (), ["REQ"])
    for k in range(len(UNP)):
        sl = slice(UB[k], UB[k + 1])
        dma("s" if k % 2 == 0 else "y", t_.REC[:, sl], t_.rec[:, sl], 2.0 + UB[k + 1] * 0.0016, (), [("REC", k)])
    dma("y", t_.MUL[:], t_.mul[:], 9.0, (), ["MUL"])
    dma("y", t_.TH[:], t_.th[:], 9.0, (), ["TH"])
    dma("s", t_.WT[:], t_.wt[:], 9.0, (), ["WT"])
    dma("s", t_.AIM[:], t_.aim[:], 9.0, (), ["AIM"])

    vset(t_.ONES[:], 1.0, 1024, ["ONES"])
    vset(t_.MSN[:], 0.0, 512, ["MSN"])
    vset(t_.MSX[:], 1.0, 512, ["MSX"])
    vset(t_.MSN[:, 0:1024:16], 65536.0, 64, ["MSN"])
    vset(t_.MSX[:, 0:1024:16], 0.0, 64, ["MSX"])
    vset(t_.C2K[:], 2048.0, 256, ["C2K"])

    def gsel(out, i, pat, op, base, cm, n, R, W_):
        add("g", [lambda: g.affine_select(out, i, pat, op, 0.0, base, cm)], 0.17 + 2 * n * CYC, R, W_)

    def gio(out, pat, base, cm, W_):
        add("g", [lambda: g.iota(out, pat, base, cm)], 0.16, (), W_)
    gsel(t_.IDP[:], t_.ONES[:, 0:128], [[-1, 128]], A.is_equal, 0, 1, 128, ["ONES"], ["IDP"])
    gsel(t_.BM0[:], t_.ONES[:, 0:128], [[-16, 8], [0, 16]], A.is_ge, 0, 1, 128, ["ONES"], ["BM0"])
    gsel(t_.BM[:], t_.BM0[:], [[16, 8], [0, 16]], A.is_ge, 15, -1, 128, ["BM0"], ["BM"])
    gio(t_.PRI[:], [[0, 16]], 0, 1, ["PRI"])
    gio(t_.I256[:], [[256, 16]], 0, 0, ["I256"])
    gio(t_.I16[:], [[16, 16]], W, 0, ["I16"])
    gsel(t_.SELA[:], t_.ONES[:], [[1, 16], [0, 8], [-1, 16]], A.is_equal, 0, 0, 2048, ["ONES"], ["SELA"])
    gsel(t_.SELC[:], t_.SELA[:], [[0, 16], [-16, 8], [0, 16]], A.is_ge, 0, 1, 2048, ["SELA"], ["SELC"])
    gsel(t_.SELB[:], t_.SELC[:], [[0, 16], [16, 8], [0, 16]], A.is_ge, 15, -1, 2048, ["SELC"], ["SELB"])
    for nm, c in (("ID4", 4096.0), ("ID7", 7.5), ("IDN", -1.0), ("IDK", 2.0 ** -13), ("IDM", -(2.0 ** -13)), ("IDH", 0.5),
                  ("IDQ", -0.25)):
        act(t_[nm][:], t_.IDP[:], F.Copy, 128, ["IDP"], [nm], scale=c)
    act(t_.BMH[:], t_.BM[:], F.Copy, 128, ["BM"], ["BMH"], scale=-0.5)

    def forms():
        vts(t_.CC[:], t_.RP[:], 4095, None, A.bitwise_and, None, 256, ["RP"], ["CC"])
        vts(t_.C16[:], t_.CC[:], -1.0, 4095.0, A.mult, A.add, 256, ["CC"], ["C16"])
        vts(t_.KK[:], t_.RP[:], 15, None, A.bitwise_and, None, 256, ["RP"], ["KK"])
        vts(t_.KM[:], t_.KK[:], -1.0, 15.0, A.mult, A.add, 256, ["KK"], tk("KM", 0, 256))
        vts(t_.A32[:], t_.RP[:], 4080, None, A.bitwise_and, None, 256, ["RP"], ["A32"])

    vts(t_.RP[:], t_.REQ[:], -1.0, -1.0, A.mult, A.add, 256, ["REQ"], ["RP"])
    forms()
    for lo, hi, e in BC0:
        spread(lo, hi, e)

    nb = [0]
    for k in range(len(UNP)):
        sl, n = slice(UB[k], UB[k + 1]), UNP[k]
        vts(t_.A2[:, sl], t_.REC[:, sl], -2047.5, 1.5 * 2.0 ** 35, A.add, A.add, n, [("REC", k)], [("A2", k)])
        act(t_.XX[:, sl], t_.A2[:, sl], F.Identity, n, [("A2", k)], [("XX", k)], bias=-1.5 * 2.0 ** 23, scale=2.0 ** -12)
        for lo in range(UB[k], UB[k + 1], 512):
            s2 = slice(lo, lo + 512)
            b, b2 = 1 + nb[0] % 3, 4 + nb[0] % 4
            nb[0] += 1
            P, P2 = t_["b%d" % b], t_["b%d" % b2]
            mm([(P[:], t_.ID7[:], t_.ONES[:, 0:512], 512, True, False), (P[:], t_.ID4[:], t_.XX[:, s2], 512, False, True)],
               ["ID7", "ID4", "ONES", ("XX", k)], b)
            vtt(t_.D7[:, s2], t_.REC[:, s2], P[:], A.subtract, 512, [("REC", k), ("ps", b)], [("D7", lo)], [b], 1.0)
            act(t_.A1[:, s2], t_.D7[:, s2], F.Identity, 512, [("D7", lo)], [("A1", lo)], bias=1.5 * 2.0 ** 27)
            act(t_.HB[:, s2], t_.A1[:, s2], F.Identity, 512, [("A1", lo)], [("HB", lo)], bias=-1.5 * 2.0 ** 27)
            mm([(P2[:], t_.ID7[:], t_.ONES[:, 0:512], 512, True, False), (P2[:], t_.IDN[:], t_.HB[:, s2], 512, False, False),
                (P2[:], t_.IDK[:], t_.HB[:, s2], 512, False, True)], ["ID7", "IDN", "IDK", "ONES", ("HB", lo)], b2)
            vtt(t_.TT[:, s2], t_.D7[:, s2], P2[:], A.add, 512, [("D7", lo), ("ps", b2)], [("TT", k)], [b2], 1.0)
    vts(t_.THH[:], t_.TH[:], 0.5, None, A.mult, None, 1, ["TH"], ["THH"])
    vcp(t_.KF[:], t_.MUL[:], 1, ["MUL"], ["KF"])
    vts(t_.KD[:], t_.IDP[:], t_.KF[:], -1.0, A.mult, A.mult, 128, ["IDP", "KF"], ["KD"], (), 0.5)
    vts(t_.PR[:], t_.PRI[:], 15, None, A.bitwise_and, None, 16, ["PRI"], ["PR"])
    vts(t_.ODC[:], t_.PR[:, 0:1], 2.0, 1.0, A.mult, A.add, 1, ["PR"], ["ODC"])
    vts(t_.OD[:], t_.IDP[:], t_.ODC[:], -1.0, A.mult, A.mult, 128, ["IDP", "ODC"], ["OD"], (), 0.5)
    vts(t_.R16[:], t_.PR[:], 16.0, None, A.mult, None, 16, ["PR"], ["R16"])
    vtt(t_.BASE[:], t_.R16[:], t_.I256[:], A.add, 16, ["R16", "I256"], ["BASE"])
    vtt(t_.DUM[:], t_.PR[:], t_.I16[:], A.add, 16, ["PR", "I16"], ["DUM"])
    vts(t_.PDC[:], t_.BASE[:], 57344.0, None, A.add, None, 16, ["BASE"], ["PDC"])
    vts(t_.DMC[:], t_.DUM[:], 57344.0, None, A.add, None, 16, ["DUM"], ["DMC"])
    vcp(t_.BH[:], t_.BM[:], 128, ["BM"], ["BH"], (), 0.5)
    vcp(t_.SELH[:], t_.SELB[:], 2048, ["SELB"], ["SELH"], (), 0.5)
    act(t_.SELM[:], t_.SELB[:], F.Copy, 2048, ["SELB"], ["SELM"], scale=-0.5)
    vts(t_.H16[:], t_.WT[:], 8.0, 16.0, A.is_ge, A.mult, 256, ["WT"], ["H16"], (), 0.5)
    vtt(t_.b0[:, 0:256], t_.WT[:], t_.H16[:], A.subtract, 256, ["WT", "H16"], ["W8"], [0])

    TTk = [("TT", k) for k in range(len(UNP))]
    XXk = [("XX", k) for k in range(len(UNP))]
    me = T.rank_of(core)

    for t in range(STEPS):
        last = t == STEPS - 1
        dst = T.cores[(me + 1 + t % 3) % len(T.cores)]
        rid, pid, _ = topo.addr(dst)
        msk, ne = topo.mask(core, dst), len(topo.engines(core, dst))
        CP, CA, TV, TA, VN, VA = [t_["%s%d" % (x, t)] for x in ("CP", "CA", "TV", "TA", "VN", "VA")]

        def send(m, out, src, R, W_, t=t, rid=rid, pid=pid, msk=msk, ne=ne, after=()):
            ls, rs = "%s%dl" % (m, t), "%s%dr" % (m, t)
            add("g", [lambda: g.remote_dma(out, src, T.sem[rs], T.sem[ls], pid, rid, msk)], SND, R, [("sent", m, t)], (), "r",
                SND, ls, ne, after)
            add("n", [], ARR, [("sent", m, t)], W_, (), "n", 0.0, rs, ne)

        for lo, hi in C1:
            m, n = hi - lo, 16 * (hi - lo)
            es, cs = slice(16 * lo, 16 * hi), slice(lo, hi)
            add("v", [lambda es=es, cs=cs: g.vector.tensor_tensor(t_.U1[:, es], t_.TT[:, 0:W].indirect(t_.C16[:, cs]),
                                                                   t_.CKB[:, es], A.subtract)],
                n * GAM * CYC + 0.05, TTk + ["C16"] + tk("CKB", lo, hi), tk("U1", lo, hi))
            act(t_.AB[:, es], t_.U1[:, es], F.Abs, n, tk("U1", lo, hi), tk("AB", lo, hi), bias=-4080.0, scale=8192.0)
            vscan(t_.MN[:, es], t_.MSN[:, 0:n], t_.AB[:, es], A.max, A.min, n, ["MSN"] + tk("AB", lo, hi), tk("MN", lo, hi))
            vtt(t_.M2[:, cs], t_.MN[:, 16 * lo + 15:16 * hi:16], t_.A32[:, cs], A.min, m, tk("MN", lo, hi) + ["A32"], tk("M2", lo, hi))
            mm([(t_.b2[:, cs], t_.IDP[:], t_.KM[:, cs], m, True, False), (t_.b2[:, cs], t_.IDN[:], t_.M2[:, cs], m, False, True)],
               ["IDP", "IDN"] + tk("KM", lo, hi) + tk("M2", lo, hi), 2)
            vts(CP[:, cs], t_.b2[:, cs], 4080.0, None, A.add, None, m, [("ps", 2)], tk(("CP", t), lo, hi), [2])
            if not last:
                mm([(t_.b3[:, cs], t_.IDP[:], t_.KM[:, cs], m, True, False), (t_.b3[:, cs], t_.IDM[:], t_.M2[:, cs], m, False, True)],
                   ["IDP", "IDM"] + tk("KM", lo, hi) + tk("M2", lo, hi), 3)
                act(TV[:, cs], t_.b3[:, cs], F.Identity, m, [("ps", 3)], tk(("TV", t), lo, hi), [3], bias=4080.0 / 8192)
            if hi in SC:
                l0 = SC[hi]
                send("e" if hi == 256 else "c", CA[:, l0:hi], CP[:, l0:hi], tk(("CP", t), l0, hi), tk(("CA", t), l0, hi))
            sgat(t_.XG[:, es], t_.XX[:, 0:W].indirect(CP[:, cs]), n, XXk + tk(("CP", t), lo, hi), tk("XG", lo, hi))
            vscan(t_.MX[:, es], t_.MSX[:, 0:n], t_.XG[:, es], A.mult, A.max, n, ["MSX"] + tk("XG", lo, hi), tk("MX", lo, hi))
            vscan(t_.MI[:, es], t_.MSN[:, 0:n], t_.XG[:, es], A.max, A.min, n, ["MSN"] + tk("XG", lo, hi), tk("MI", lo, hi))
            lc = slice(16 * lo + 15, 16 * hi, 16)
            mm([(t_.b1[:, cs], t_.IDQ[:], t_.ONES[:, 0:m], m, True, False), (t_.b1[:, cs], t_.IDH[:], t_.MX[:, lc], m, False, False),
                (t_.b1[:, cs], t_.IDH[:], t_.MI[:, lc], m, False, True)], ["IDQ", "IDH", "ONES"] + tk("MX", lo, hi) + tk("MI", lo, hi), 1)
            vts(t_.Z[:, cs], t_.b1[:, cs], 1.5 * 2.0 ** 23, -1.5 * 2.0 ** 23, A.add, A.add, m, [("ps", 1)], tk("Z", lo, hi), [1])
            mm([(t_.b3[:, cs], t_.IDP[:], t_.Z[:, cs], m, True, False), (t_.b3[:, cs], t_.IDN[:], t_.AIM[:, cs], m, False, True)],
               ["IDP", "IDN", "AIM"] + tk("Z", lo, hi), 3)
            act(VN[:, cs], t_.b3[:, cs], F.Abs, m, [("ps", 3)], tk(("VN", t), lo, hi), [3])
            if hi in SV and hi < 256:
                send("v", VA[:, SV[hi]:hi], VN[:, SV[hi]:hi], tk(("VN", t), SV[hi], hi), tk(("VA", t), SV[hi], hi))
            vtt(t_.WZ[:, cs], t_.b0[:, cs], t_.Z[:, cs], A.mult, m, ["W8"] + tk("Z", lo, hi), tk("WZ", lo, hi), [0], 1.0)
            ps = t_.b4[:, 256 + lo // 16:256 + hi // 16]
            mm([(ps, t_.SELH[:, 128 * r:128 * r + 128], t_.WZ[:, lo + r:hi:16], m // 16, r == 0, r == 15) for r in range(16)],
               ["SELH"] + tk("WZ", lo, hi), 4)
        vcp(t_.N32[:], t_.b4[:, 256:272], 16, [("ps", 4)], ["N32"], [4])
        vts(t_.N15[:], t_.N32[:], 15, None, A.bitwise_and, None, 16, ["N32"], ["N15"])
        vtt(t_.PI[:], t_.N15[:], t_.BASE[:], A.add, 16, ["N15", "BASE"], ["PI"])
        vcp(t_.P16[:], t_.PI[:], 16, ["PI"], ["P16"])
        vscat(t_.XX[:, 0:WP].indirect(t_.P16[:]), VN[:, 0:256], 256, ["P16"] + tk(("VN", t), 0, 256), XXk)
        vcp(VN[:, 256:272], t_.N15[:], 16, ["N15"], tk(("VN", t), 256, 272))
        l0 = SV[256]
        send("w", VA[:, l0:272], VN[:, l0:272], tk(("VN", t), l0, 272), tk(("VA", t), l0, 272))
        if not last:
            send("t", TA[:], TV[:], tk(("TV", t), 0, 256), [("TA", t)], after=[len(ops) - 2])
            vscat(t_.TT[:, 0:WP].indirect(t_.P16[:]), TV[:], 256, ["P16"] + tk(("TV", t), 0, 256), TTk)
        for hi in SV:
            l0 = SV[hi]
            vcp(t_.b0[:, 256 + l0:256 + hi], VA[:, l0:hi], hi - l0, tk(("VA", t), l0, hi), tk("VAP", l0, hi), [0])
        vtt(t_.PD[:], VA[:, 256:272], t_.PDC[:], A.add, 16, tk(("VA", t), 256, 272) + ["PDC"], ["PD"])
        if last:
            dma("y", t_.yz[:], t_.Z[:], 2.5, tk("Z", 0, 256), ["yz"])
        for c in range(len(C3)):
            lo, hi = C3[c]
            n, m = 16 * (hi - lo), hi - lo
            es, cs = slice(16 * lo, 16 * hi), slice(lo, hi)
            sgat(t_.XA[:, es], t_.XX[:, 0:W].indirect(CA[:, cs]), n, XXk + tk(("CA", t), lo, hi), tk("XA", lo, hi))
            bd = 6 + c % 2
            D = t_["b%d" % bd][:, cs]
            if c in AC:
                for h in range(2):
                    P = t_["b%d" % (2 + h)]
                    mm([x for j in range(8) for x in
                        ((P[:, m * j:m * j + m], t_.IDP[:], t_.XA[:, 16 * lo + 8 * h + j:16 * hi:16], m, True, False),
                         (P[:, m * j:m * j + m], t_.IDN[:], VA[:, cs], m, False, True))],
                       ["IDP", "IDN"] + tk("XA", lo, hi) + tk(("VA", t), lo, hi), 2 + h)
                    a0 = 16 * lo + 8 * m * h
                    act(t_.MXA[:, a0:a0 + 8 * m], P[:, 0:8 * m], F.Abs, 8 * m, [("ps", 2 + h)], [("MXB", lo, h)], [2 + h], scale=0.5)
                mm([(D, t_.SELB[:, 128 * j:128 * j + 128], t_.MXA[:, 16 * lo + m * j:16 * lo + m * j + m], m, j == 0, j == 15)
                    for j in range(16)], ["SELB", ("MXB", lo, 0), ("MXB", lo, 1)], bd)
            else:
                add("v", [(lambda j=j, lo=lo, hi=hi: g.vector.tensor_tensor(t_.MXA[:, 16 * lo + j:16 * hi:16],
                           t_.XA[:, 16 * lo + j:16 * hi:16], t_.b0[:, 256 + lo:256 + hi], A.max)) for j in range(16)],
                    16 * max(64, m) * CYC, tk("XA", lo, hi) + tk("VAP", lo, hi), tk("MXA", lo, hi), [0])
                mm([(D, t_.BMH[:], VA[:, cs], m, True, False)] +
                   [(D, t_.SELM[:, 128 * j:128 * j + 128], t_.XA[:, 16 * lo + j:16 * hi:16], m, False, False) for j in range(16)],
                   ["BMH", "SELM"] + tk(("VA", t), lo, hi) + tk("XA", lo, hi), bd)
                mm([(D, t_.SELB[:, 128 * j:128 * j + 128], t_.MXA[:, 16 * lo + j:16 * hi:16], m, False, j == 15) for j in range(16)],
                   ["SELB"] + tk("MXA", lo, hi), bd)
            vts(t_.FL[:, cs], D, t_.THH[:], 8192.0, A.is_ge, A.mult, m, [("ps", bd), "THH"], tk("FL", lo, hi), [bd])
            if c not in KG:
                continue
            lo = C3[KG[c]][0]
            m, cs = hi - lo, slice(lo, hi)
            w = slice(lo // 16, hi // 16)
            mm([(t_.b1[:, w], t_.SELB[:, 128 * r:128 * r + 128], t_.FL[:, lo + r:hi:16], m // 16, r == 0, r == 15) for r in range(16)],
               ["SELB"] + tk("FL", lo, hi), 1)
            vtt(t_.OF[:, w], t_.b1[:, w], t_.PD[:, w], A.max, 4, [("ps", 1), "PD"], [("OF", c)], [1])
            vtt(t_.OG[:, w], t_.OF[:, w], t_.DMC[:, w], A.min, 4, [("OF", c), "DMC"], [("OG", c)])
            vts(t_.O16[:, w], t_.OG[:, w], -57344.0, None, A.add, None, 4, [("OG", c)], [("O16", c)])
            if not last:
                vscat(t_.TT[:, 0:WP].indirect(t_.O16[:, w]), TA[:, cs], m, [("O16", c), ("TA", t)], TTk)
        vscat(t_.XX[:, 0:WP].indirect(t_.O16[:]), VA[:, 0:256], 256, [("O16", c) for c in KG] + tk(("VA", t), 0, 256), XXk)
        Zt, Wt = tk("Z", 0, 256), tk("WZ", 0, 256)
        vtt(t_.HZ[:], t_.H16[:], t_.Z[:], A.mult, 256, ["H16"] + Zt, ["HZ"])
        mm([(t_.b4[:, 0:256], t_.BM[:], t_.HZ[:], 256, True, False), (t_.b4[:, 0:256], t_.BH[:], t_.WZ[:], 256, False, True)],
           ["BM", "BH", "HZ"] + Wt, 4)
        vcp(t_.UI[:], t_.b4[:, 0:256], 256, [("ps", 4)], ["UI"], [4])
        vts(t_.UU[:], t_.UI[:], 4095, None, A.bitwise_and, None, 256, ["UI"], ["UU"])
        vts(t_.UM[:], t_.UU[:], -2048.0, None, A.add, None, 256, ["UU"], ["UM"])
        vtt(t_.SQ[:], t_.UU[:], t_.UU[:], A.mult, 256, ["UU"], ["SQ"])
        vts(t_.FF[:], t_.SQ[:], 5, None, A.arith_shift_right, None, 256, ["SQ"], ["FF"])
        G = t_.b5[:, 0:256]
        mm([(G, t_.IDN[:], t_.ONES[:, 0:256], 256, True, False), (G, t_.OD[:], t_.Z[:], 256, False, False),
            (G, t_.KD[:], t_.C2K[:], 256, False, False), (G, t_.KD[:], t_.UM[:], 256, False, True)],
           ["IDN", "ONES", "OD", "KD", "C2K", "UM"] + Zt, 5)
        vtt(t_.RP[:], G, t_.FF[:], A.subtract, 256, ["FF", ("ps", 5)], ["RP"], [5], 1.0)
        if last:
            vts(t_.CC[:], t_.RP[:], 4095, None, A.bitwise_and, None, 256, ["RP"], ["CC"])
            vts(t_.YC[:], t_.CC[:], -1.0, 4095.0, A.mult, A.add, 256, ["CC"], ["YC"])
            dma("y", t_.yc[:], t_.YC[:], 2.5, ["YC"], ["yc"])
        else:
            forms()
            for lo, hi, e in BCN:
                spread(lo, hi, e)
    dma("y", t_.yx[:], t_.XX[:, 0:W], 5.0, XXk, ["yx"])
    return ops, q


def rank_program(g, core, T, topo):
    if T.rank_of(core) is None:
        return
    ops, q = build(g, T, core, topo)
    preds = plan(ops)
    if "o" not in ORDER:
        ORDER["o"] = schedule(ops, preds)
    order = ORDER["o"][0]
    pos = {}
    for i in order:
        pos[i] = len(pos)
    semof = {"v": "sv", "s": "ss", "t": "st", "g": "sg"}
    cnt, done, clock, final = {}, {}, {}, {}
    known = {e: {} for e in q}
    for i in order:
        o = ops[i]
        e = o["e"]
        if e == "n":
            done[i] = (o["sem"], o["val"])
            final[o["sem"]] = o["val"]
            clock[i] = {}
            continue
        kn = known[e]
        for j in sorted(preds[i], key=lambda x: -pos[x]):
            if not preds[i][j]:
                continue
            s, v = done[j]
            if kn.get(s, 0) >= v:
                continue
            q[e].wait_ge(T.sem[s], v)
            kn[s] = v
            for a, b in clock[j].items():
                if kn.get(a, 0) < b:
                    kn[a] = b
        clock[i] = dict(kn)
        if o["k"] == "c":
            s = semof[e]
            for f in o["f"]:
                f().then_inc(T.sem[s], 1)
                cnt[s] = cnt.get(s, 0) + 1
            done[i] = (s, cnt[s])
        elif o["k"] == "d":
            o["f"][0]().then_inc(T.sem[o["sem"]], 16)
            done[i] = (o["sem"], 16)
        else:
            o["f"][0]()
            done[i] = (o["sem"], o["val"])
        final[done[i][0]] = done[i][1]
        clock[i][done[i][0]] = done[i][1]
    for s in sorted(final):
        if known["g"].get(s, 0) < final[s]:
            g.wait_ge(T.sem[s], final[s])
